import numpy as np
import ml_dtypes


def mxq(x, axis, fmt="e4m3"):
    dtype, down = {"e4m3": (ml_dtypes.float8_e4m3fn, 7), "e5m2": (ml_dtypes.float8_e5m2, 14)}[fmt]
    v = np.moveaxis(np.asarray(x, np.float32).astype(ml_dtypes.bfloat16).astype(np.float64), axis, -1)
    blocks = v.reshape(v.shape[:-1] + (-1, 32))
    amax = np.abs(blocks).max(-1, keepdims=True)
    byte = np.maximum(np.where(amax > 0, np.frexp(amax)[1] - 1 + 127, 0) - down, 1)
    scale = np.exp2(byte - 127.0)
    codes = (blocks / scale).astype(np.float32).astype(dtype).astype(np.float64)
    return np.moveaxis((codes * scale).reshape(v.shape), -1, axis)


WIDE = False


def mx_kscale(k):
    if not WIDE:
        return np.ones(k)
    levels = np.array([10, -10, 5, -5, 0])
    if k % 512:
        return np.exp2(np.random.permutation(np.resize(levels, k // 32))).repeat(32)
    a = np.empty((k // 512, 16))
    for p in range(k // 512):
        a[p, :8] = np.random.permutation(np.resize(levels, 8))
        for g in range(8):
            far = levels[np.abs(levels - a[p, g]) >= 10]
            a[p, g + 8] = far[np.random.randint(len(far))]
    return np.exp2(a.ravel()).repeat(32)


def f64(x):
    return np.asarray(x).astype(np.float64)


def striped(idx):
    return np.tile(idx.reshape(-1, 16).T, (8, 1)).astype(np.uint16)


def unstriped(offs):
    return offs[:16].T.reshape(-1).astype(np.int64)


def silu(v):
    return v / (1.0 + np.exp(-np.maximum(v, -700.0)))


K, T, D, S, V, N = 1024, 2048, 3, 512, 256, 512


def setup_inputs():
    n = np.random.standard_normal
    s = mx_kscale(K)[:, None]
    return {
        "xT": (n((K, T)) * s).astype(np.float32),
        "w": (n((K, N)) / np.sqrt(K) / s).astype(np.float32),
        "b": (0.3 * n((N, 1))).astype(np.float32),
        "gate": np.tile(np.random.uniform(0.2, 1.0, (D, 1, V)) / np.sqrt(D), (1, N, 1)).astype(np.float32),
        "offs": striped(np.random.permutation(T)[:S]),
        "pos1": striped(np.random.permutation(S)[:V]),
        "pos2": striped(np.random.permutation(S)[:V]),
        "pos3": striped(np.random.permutation(S)[:V]),
    }


def reference(xT, w, b, gate, offs, pos1, pos2, pos3):
    idx = unstriped(offs)
    xq = mxq(f64(xT)[:, idx], 0, "e4m3")
    y = mxq(f64(w), 0, "e4m3").T @ xq
    y = silu(y + f64(b))
    return sum(f64(gate[d]) * y[:, unstriped(p)] for d, p in enumerate((pos1, pos2, pos3)))

@@ -1,0 +1,218 @@
+from contextlib import ExitStack
+
+import concourse.mybir as mybir
+
+K, T, D, S, V, N = 1024, 2048, 3, 512, 256, 512
+FLOPS = 2 * K * S * N
+
+F32 = mybir.dt.float32
+BF16 = mybir.dt.bfloat16
+U32 = mybir.dt.uint32
+U16 = mybir.dt.uint16
+U8 = mybir.dt.uint8
+FP8X4 = mybir.dt.float8_e4m3fn_x4
+MULT = mybir.AluOpType.mult
+ADD = mybir.AluOpType.add
+SILU = mybir.ActivationFunctionType.Silu
+
+P = 128
+PACK = 4
+K_PASS = P * PACK
+PASSES = K // K_PASS
+BLOCKS = N // P
+PIECES = [(0, 256), (256, 384), (384, 512)]
+
+
+def tile_picked_sub_lin_silu_sub_e_kernel(tc, xT, w, b, gate, offs, pos1, pos2, pos3, out):
+    nc = tc.nc
+    with ExitStack() as ctx:
+        lists = ctx.enter_context(tc.tile_pool(name="lists", bufs=1))
+        keep = ctx.enter_context(tc.tile_pool(name="keep", bufs=1))
+        psum = ctx.enter_context(tc.psum_pool(name="psum", bufs=1))
+
+        offs_sb = lists.tile([P, S // 16], U16, name="offs_sb")
+        nc.sync.dma_start(offs_sb[:], offs)
+
+        b_rows = keep.tile([P, 32], F32, name="b_rows", align_bytes=64)
+        nc.vector.memset(b_rows[:], 0.0)
+        warm = keep.tile([P, 8], F32, name="warm")
+        nc.gpsimd.memset(warm[:], 0.0)
+        warmed = keep.tile([P, 8], F32, name="warmed")
+        nc.scalar.activation(warmed[:], warm[:], SILU)
+
+        def load_bias():
+            for c in range(BLOCKS):
+                nc.sync.dma_start(
+                    b_rows[c:P:32, :], b[c * P : (c + 1) * P, :].rearrange("(q i) o -> q (i o)", i=32)
+                )
+
+        planes = {}
+        for a, j0, count in ((0, 0, 1), (0, 1, 1), (0, 2, 1), (0, 3, 1), (1, 0, 1), (1, 1, 1), (1, 2, 1), (1, 3, 1)):
+            if (a, j0) == (1, 0):
+                load_bias()
+            rows = xT[a * K_PASS : (a + 1) * K_PASS, :].rearrange("(p j) t -> p j t", j=PACK)
+            group = keep.tile([P, count, T], F32, name=f"x{a}{j0}")
+            nc.sync.dma_start(group[:], rows[:, j0 : j0 + count, :])
+            for j in range(count):
+                planes[a, j0 + j] = group[:, j, :]
+
+        raws = {}
+
+        def load_w(a, c, blocks):
+            raw = keep.tile([P, PACK, blocks * P], F32, name=f"wraw{a}{c}")
+            rows = w[a * K_PASS : (a + 1) * K_PASS, c * P : (c + blocks) * P]
+            nc.sync.dma_start(raw[:], rows.rearrange("(p j) m -> p j m", j=PACK))
+            raws[a, c] = raw
+
+        gates = []
+
+        def load_gate(c):
+            g = keep.tile([P, D, V], F32, name=f"gate{c}")
+            nc.sync.dma_start(g[:], gate[:, c * P : (c + 1) * P, :].rearrange("d m v -> m d v"))
+            gates.append(g)
+
+        for c in (0, 1):
+            for a in range(PASSES):
+                load_w(a, c, 1)
+        pos_sb = []
+        for d, pos in enumerate((pos1, pos2, pos3)):
+            pos_tile = lists.tile([P, V // 16], U16, name=f"pos_sb{d}")
+            nc.sync.dma_start(pos_tile[:], pos)
+            pos_sb.append(pos_tile)
+        load_gate(0)
+        for a in range(PASSES):
+            load_w(a, 2, 2)
+        for c in range(1, BLOCKS):
+            load_gate(c)
+
+        xb, xq, xs = [], [], []
+        for a in range(PASSES):
+            xb.append(keep.tile([P, S, PACK], BF16, name=f"xb{a}", align_bytes=64))
+            xq.append(keep.tile([P, S], U32, name=f"xq{a}", align_bytes=64))
+            xs.append(keep.tile([P, S], U8, name=f"xs{a}", align_bytes=64))
+        picked = [keep.tile([P, PACK, S], F32, name=f"picked{a}") for a in range(PASSES)]
+
+        def gather_wide(a, j):
+            nc.vector.tensor_copy(picked[a][:, j, :], planes[a, j].indirect(offs_sb[:]))
+
+        def gather(a, j, lo, hi):
+            nc.vector.tensor_copy(xb[a][:, lo:hi, j], planes[a, j].indirect(offs_sb[:, lo // 16 : hi // 16]))
+
+        def interleave_x(a, j0, j1, lo, hi):
+            nc.scalar.copy(
+                xb[a][:, lo:hi, j0:j1], picked[a][:, j0:j1, lo:hi].rearrange("p j s -> p s j")
+            )
+
+        def quantise_x(a, lo, hi):
+            nc.vector.quantize_mx(
+                out=xq[a][:, lo:hi].bitcast(FP8X4),
+                scales=xs[a][:, lo:hi],
+                in_=xb[a][:, lo:hi, :].rearrange("p s j -> p (s j)"),
+            )
+
+        for j in range(PACK):
+            gather_wide(0, j)
+        for lo in (0, S // 2):
+            interleave_x(0, 0, PACK, lo, lo + S // 2)
+        gather_wide(1, 0)
+        gather_wide(1, 1)
+        interleave_x(1, 0, 2, 0, S)
+        quantise_x(0, 0, S)
+        gather(1, 2, 0, S)
+        gather(1, 3, 0, S // 2)
+        gather(1, 3, S // 2, S)
+        for lo, hi in PIECES:
+            quantise_x(1, lo, hi)
+
+        bias = keep.tile([P, 32], F32, name="bias", align_bytes=64)
+        nc.vector.transpose(bias[:], b_rows[:])
+
+        weights = {}
+
+        def prepare_w(c, blocks, joined):
+            m = blocks * P
+            wq = keep.tile([P, PASSES, m], U32, name=f"wq{c}", align_bytes=64)
+            ws = keep.tile([P, PASSES, m], U8, name=f"ws{c}", align_bytes=64)
+            wb = keep.tile([P, PASSES, m, PACK], BF16, name=f"wb{c}", align_bytes=64)
+            for a in range(PASSES):
+                nc.scalar.copy(
+                    wb[:, a].rearrange("p (g i) j -> p g j i", i=4),
+                    raws[a, c][:].rearrange("p j (g i) -> p g j i", i=4),
+                )
+                if not joined:
+                    nc.vector.quantize_mx(
+                        out=wq[:, a].bitcast(FP8X4), scales=ws[:, a], in_=wb[:, a].rearrange("p m j -> p (m j)")
+                    )
+            if joined:
+                nc.vector.quantize_mx(
+                    out=wq[:].rearrange("p a m -> p (a m)").bitcast(FP8X4),
+                    scales=ws[:].rearrange("p a m -> p (a m)"),
+                    in_=wb[:].rearrange("p a m j -> p (a m j)"),
+                )
+            for i in range(blocks):
+                for a in range(PASSES):
+                    weights[c + i, a] = (wq[:, a, i * P : (i + 1) * P], ws[:, a, i * P : (i + 1) * P])
+
+        def results(c, pieces):
+            y = keep.tile([P, S], F32, name=f"y{c}")
+            for lo, hi in pieces:
+                acc = psum.tile([P, hi - lo], F32, name=f"acc{c}{lo}")
+                for a in range(PASSES):
+                    wq, ws = weights[c, a]
+                    nc.tensor.matmul_mx(
+                        out=acc[:],
+                        lhsT=wq.bitcast(FP8X4),
+                        lhsT_scale=ws,
+                        rhs=xq[a][:, lo:hi].bitcast(FP8X4),
+                        rhs_scale=xs[a][:, lo:hi],
+                        start=(a == 0),
+                        stop=(a == PASSES - 1),
+                    )
+                nc.scalar.activation(y[:, lo:hi], acc[:], SILU, bias=bias[:, c : c + 1])
+            ys.append(y)
+
+        ys = []
+        prepare_w(0, 1, False)
+        results(0, PIECES)
+        prepare_w(1, 1, True)
+        results(1, [(0, S)])
+
+        terms, sums, outs = {}, {}, {}
+        for c0, count in ((0, 2), (2, 1), (3, 1)):
+            terms[c0] = keep.tile([P, count, D, V], F32, name=f"terms{c0}")
+            sums[c0] = keep.tile([P, count, V], F32, name=f"sums{c0}")
+            outs[c0] = keep.tile([P, count, V], F32, name=f"outs{c0}")
+
+        def fetch(c, d, c0):
+            nc.vector.tensor_tensor(
+                terms[c0][:, c - c0, d, :], ys[c][:].indirect(pos_sb[d][:]), gates[c][:, d, :], MULT
+            )
+
+        def add_first(c0):
+            nc.vector.tensor_tensor(sums[c0][:], terms[c0][:, :, 0, :], terms[c0][:, :, 1, :], ADD)
+
+        def add_last(c0, count):
+            nc.vector.tensor_tensor(outs[c0][:], sums[c0][:], terms[c0][:, :, 2, :], ADD)
+            rows = out[c0 * P : (c0 + count) * P, :]
+            nc.sync.dma_start(rows.rearrange("(c p) v -> p c v", p=P), outs[c0][:])
+
+        fetch(0, 0, 0)
+        fetch(0, 1, 0)
+        prepare_w(2, 2, True)
+        results(2, [(0, S)])
+        results(3, [(0, S)])
+        fetch(0, 2, 0)
+        for d in range(D):
+            fetch(1, d, 0)
+        fetch(2, 0, 2)
+        add_first(0)
+        fetch(2, 1, 2)
+        add_last(0, 2)
+        fetch(2, 2, 2)
+        fetch(3, 0, 3)
+        add_first(2)
+        fetch(3, 1, 3)
+        fetch(3, 2, 3)
+        add_first(3)
+        add_last(2, 1)
+        add_last(3, 1)

@@ -1,6 +1,7 @@
 from contextlib import ExitStack
 
 import concourse.mybir as mybir
+from concourse.masks import make_identity
 
 K, T, D, S, V, N = 1024, 2048, 3, 512, 256, 512
 FLOPS = 2 * K * S * N
@@ -20,7 +21,8 @@ PACK = 4
 K_PASS = P * PACK
 PASSES = K // K_PASS
 BLOCKS = N // P
-PIECES = [(0, 256), (256, 384), (384, 512)]
+HALVES = [(0, S // 2), (S // 2, S)]
+PIECES = [(0, 128), (128, 256), (256, 512)]
 
 
 def tile_picked_sub_lin_silu_sub_e_kernel(tc, xT, w, b, gate, offs, pos1, pos2, pos3, out):
@@ -31,20 +33,19 @@ def tile_picked_sub_lin_silu_sub_e_kernel(tc, xT, w, b, gate, offs, pos1, pos2, 
         psum = ctx.enter_context(tc.psum_pool(name="psum", bufs=1))
 
         offs_sb = lists.tile([P, S // 16], U16, name="offs_sb")
-        nc.sync.dma_start(offs_sb[:], offs)
 
-        b_rows = keep.tile([P, 32], F32, name="b_rows", align_bytes=64)
-        nc.vector.memset(b_rows[:], 0.0)
+        rows_sb = keep.tile([P, V], F32, name="rows_sb")
+        nc.gpsimd.memset(rows_sb[:], 0.0)
+        ident = keep.tile([P, P], F32, name="ident")
+        make_identity(nc, ident[:])
         warm = keep.tile([P, 8], F32, name="warm")
         nc.gpsimd.memset(warm[:], 0.0)
         warmed = keep.tile([P, 8], F32, name="warmed")
         nc.scalar.activation(warmed[:], warm[:], SILU)
 
         def load_bias():
-            for c in range(BLOCKS):
-                nc.sync.dma_start(
-                    b_rows[c:P:32, :], b[c * P : (c + 1) * P, :].rearrange("(q i) o -> q (i o)", i=32)
-                )
+            nc.sync.dma_start(rows_sb[0:D, :], gate[:, 0, :])
+            nc.sync.dma_start(rows_sb[4:6, :], b.rearrange("(r i) o -> r (i o)", i=V))
 
         planes = {}
         for a, j0, count in ((0, 0, 1), (0, 1, 1), (0, 2, 1), (0, 3, 1), (1, 0, 1), (1, 1, 1), (1, 2, 1), (1, 3, 1)):
@@ -53,23 +54,18 @@ def tile_picked_sub_lin_silu_sub_e_kernel(tc, xT, w, b, gate, offs, pos1, pos2, 
             rows = xT[a * K_PASS : (a + 1) * K_PASS, :].rearrange("(p j) t -> p j t", j=PACK)
             group = keep.tile([P, count, T], F32, name=f"x{a}{j0}")
             nc.sync.dma_start(group[:], rows[:, j0 : j0 + count, :])
+            if (a, j0) == (0, 0):
+                nc.sync.dma_start(offs_sb[:], offs)
             for j in range(count):
                 planes[a, j0 + j] = group[:, j, :]
 
         raws = {}
 
         def load_w(a, c, blocks):
-            raw = keep.tile([P, PACK, blocks * P], F32, name=f"wraw{a}{c}")
+            raw = keep.tile([P, PACK, blocks * P], F32, name=f"wraw{a}{c}", align_bytes=64)
             rows = w[a * K_PASS : (a + 1) * K_PASS, c * P : (c + blocks) * P]
             nc.sync.dma_start(raw[:], rows.rearrange("(p j) m -> p j m", j=PACK))
             raws[a, c] = raw
-
-        gates = []
-
-        def load_gate(c):
-            g = keep.tile([P, D, V], F32, name=f"gate{c}")
-            nc.sync.dma_start(g[:], gate[:, c * P : (c + 1) * P, :].rearrange("d m v -> m d v"))
-            gates.append(g)
 
         for c in (0, 1):
             for a in range(PASSES):
@@ -79,17 +75,15 @@ def tile_picked_sub_lin_silu_sub_e_kernel(tc, xT, w, b, gate, offs, pos1, pos2, 
             pos_tile = lists.tile([P, V // 16], U16, name=f"pos_sb{d}")
             nc.sync.dma_start(pos_tile[:], pos)
             pos_sb.append(pos_tile)
-        load_gate(0)
-        for a in range(PASSES):
-            load_w(a, 2, 2)
-        for c in range(1, BLOCKS):
-            load_gate(c)
+        for c in (2, 3):
+            for a in range(PASSES):
+                load_w(a, c, 1)
 
         xb, xq, xs = [], [], []
         for a in range(PASSES):
             xb.append(keep.tile([P, S, PACK], BF16, name=f"xb{a}", align_bytes=64))
-            xq.append(keep.tile([P, S], U32, name=f"xq{a}", align_bytes=64))
             xs.append(keep.tile([P, S], U8, name=f"xs{a}", align_bytes=64))
+        xq.append(keep.tile([P, S], U32, name="xq0", align_bytes=64))
         picked = [keep.tile([P, PACK, S], F32, name=f"picked{a}") for a in range(PASSES)]
 
         def gather_wide(a, j):
@@ -114,49 +108,63 @@ def tile_picked_sub_lin_silu_sub_e_kernel(tc, xT, w, b, gate, offs, pos1, pos2, 
             gather_wide(0, j)
         for lo in (0, S // 2):
             interleave_x(0, 0, PACK, lo, lo + S // 2)
+        turned = psum.tile([P, 2, P], F32, name="turned", tag="acc3")
+        for h in range(2):
+            nc.tensor.transpose(turned[:, h, :], rows_sb[:, h * P : (h + 1) * P], ident[:])
+        cols = keep.tile([P, 2, 8], F32, name="cols")
+        nc.scalar.copy(cols[:], turned[:, :, 0:8])
+        gate_sb = keep.tile([P, D, V], F32, name="gate_sb")
+        for d0, count in ((0, 2), (2, 1)):
+            spread = psum.tile([P, count, V], F32, name=f"spread{d0}")
+            for d in range(count):
+                for h in range(2):
+                    nc.tensor.transpose(
+                        spread[:, d, h * P : (h + 1) * P],
+                        cols[:, h, d0 + d : d0 + d + 1].to_broadcast([P, P]),
+                        ident[:],
+                    )
+            nc.scalar.copy(gate_sb[:, d0 : d0 + count, :], spread[:])
         gather_wide(1, 0)
         gather_wide(1, 1)
         interleave_x(1, 0, 2, 0, S)
         quantise_x(0, 0, S)
         gather(1, 2, 0, S)
-        gather(1, 3, 0, S // 2)
-        gather(1, 3, S // 2, S)
-        for lo, hi in PIECES:
-            quantise_x(1, lo, hi)
-
-        bias = keep.tile([P, 32], F32, name="bias", align_bytes=64)
-        nc.vector.transpose(bias[:], b_rows[:])
-
+        gather(1, 3, 0, S)
         weights = {}
 
-        def prepare_w(c, blocks, joined):
-            m = blocks * P
-            wq = keep.tile([P, PASSES, m], U32, name=f"wq{c}", align_bytes=64)
-            ws = keep.tile([P, PASSES, m], U8, name=f"ws{c}", align_bytes=64)
-            wb = keep.tile([P, PASSES, m, PACK], BF16, name=f"wb{c}", align_bytes=64)
-            for a in range(PASSES):
-                nc.scalar.copy(
-                    wb[:, a].rearrange("p (g i) j -> p g j i", i=4),
-                    raws[a, c][:].rearrange("p j (g i) -> p g j i", i=4),
-                )
-                if not joined:
-                    nc.vector.quantize_mx(
-                        out=wq[:, a].bitcast(FP8X4), scales=ws[:, a], in_=wb[:, a].rearrange("p m j -> p (m j)")
-                    )
-            if joined:
-                nc.vector.quantize_mx(
-                    out=wq[:].rearrange("p a m -> p (a m)").bitcast(FP8X4),
-                    scales=ws[:].rearrange("p a m -> p (a m)"),
-                    in_=wb[:].rearrange("p a m j -> p (a m j)"),
-                )
-            for i in range(blocks):
-                for a in range(PASSES):
-                    weights[c + i, a] = (wq[:, a, i * P : (i + 1) * P], ws[:, a, i * P : (i + 1) * P])
+        def interleave_w(dst, a, c):
+            copy = nc.vector.tensor_copy if c == 1 else nc.scalar.copy
+            copy(
+                dst.rearrange("p (g i) j -> p g j i", i=4),
+                raws[a, c][:].rearrange("p j (g i) -> p g j i", i=4),
+            )
 
-        def results(c, pieces):
-            y = keep.tile([P, S], F32, name=f"y{c}")
-            for lo, hi in pieces:
-                acc = psum.tile([P, hi - lo], F32, name=f"acc{c}{lo}")
+        def prepare_pass(c, a, slot):
+            wq = keep.tile([P, P], U32, name=f"wq{c}{a}", align_bytes=64)
+            ws = keep.tile([P, P], U8, name=f"ws{c}{a}", align_bytes=64)
+            wb = keep.tile([P, P, PACK], BF16, name=f"wb{c}{a}", tag=slot, align_bytes=64)
+            interleave_w(wb[:], a, c)
+            nc.vector.quantize_mx(out=wq[:].bitcast(FP8X4), scales=ws[:], in_=wb[:].rearrange("p m j -> p (m j)"))
+            weights[c, a] = (wq[:], ws[:])
+
+        def prepare_w(c, slot):
+            wq = keep.tile([P, PASSES, P], U32, name=f"wq{c}", align_bytes=64)
+            ws = keep.tile([P, PASSES, P], U8, name=f"ws{c}", align_bytes=64)
+            wb = keep.tile([P, PASSES, P, PACK], BF16, name=f"wb{c}", tag=slot, align_bytes=64)
+            for a in range(PASSES):
+                interleave_w(wb[:, a], a, c)
+            nc.vector.quantize_mx(
+                out=wq[:].rearrange("p a m -> p (a m)").bitcast(FP8X4),
+                scales=ws[:].rearrange("p a m -> p (a m)"),
+                in_=wb[:].rearrange("p a m j -> p (a m j)"),
+            )
+            for a in range(PASSES):
+                weights[c, a] = (wq[:, a, :], ws[:, a, :])
+
+        def results(c, pieces, banks):
+            y = keep.tile([P, S], F32, name=f"y{c}", tag="wraw12" if c == 1 else f"y{c}", align_bytes=64)
+            for (lo, hi), bank in zip(pieces, banks):
+                acc = psum.tile([P, hi - lo], F32, name=f"acc{c}{lo}", tag=bank)
                 for a in range(PASSES):
                     wq, ws = weights[c, a]
                     nc.tensor.matmul_mx(
@@ -168,51 +176,71 @@ def tile_picked_sub_lin_silu_sub_e_kernel(tc, xT, w, b, gate, offs, pos1, pos2, 
                         start=(a == 0),
                         stop=(a == PASSES - 1),
                     )
-                nc.scalar.activation(y[:, lo:hi], acc[:], SILU, bias=bias[:, c : c + 1])
+                nc.scalar.activation(y[:, lo:hi], acc[:], SILU, bias=cols[:, c % 2, 4 + c // 2 : 5 + c // 2])
             ys.append(y)
 
         ys = []
-        prepare_w(0, 1, False)
-        results(0, PIECES)
-        prepare_w(1, 1, True)
-        results(1, [(0, S)])
+        prepare_pass(0, 0, "wb00")
+        xq.append(keep.tile([P, S], U32, name="xq1", tag="wraw00", align_bytes=64))
+        quantise_x(1, 0, S)
+        prepare_pass(0, 1, "wb01")
+        results(0, PIECES, ("acc0", "piece128", "piece256"))
+        prepare_w(1, "wraw10")
+        prepare_pass(2, 0, "wq01")
+        prepare_pass(2, 1, "wb21")
+        results(1, [(0, S)], ("acc1",))
+        prepare_pass(3, 0, "wq1")
+        prepare_pass(3, 1, "wb31")
+        results(2, HALVES, ("acc2", "acc0"))
+        results(3, HALVES, ("acc3", "acc1"))
 
-        terms, sums, outs = {}, {}, {}
-        for c0, count in ((0, 2), (2, 1), (3, 1)):
-            terms[c0] = keep.tile([P, count, D, V], F32, name=f"terms{c0}")
-            sums[c0] = keep.tile([P, count, V], F32, name=f"sums{c0}")
-            outs[c0] = keep.tile([P, count, V], F32, name=f"outs{c0}")
+        terms = {}
+        slots = {(0, 2): "wraw02", (1, 1): "wraw03", (1, 2): "wraw13"}
 
-        def fetch(c, d, c0):
-            nc.vector.tensor_tensor(
-                terms[c0][:, c - c0, d, :], ys[c][:].indirect(pos_sb[d][:]), gates[c][:, d, :], MULT
-            )
+        def fetch(c, d):
+            term = keep.tile([P, V], F32, name=f"term{c}{d}", tag=slots.get((c, d), f"term{c}{d}"), align_bytes=64)
+            nc.vector.tensor_tensor(term[:], ys[c][:].indirect(pos_sb[d][:]), gate_sb[:, d, :], MULT)
+            terms[c, d] = term
 
-        def add_first(c0):
-            nc.vector.tensor_tensor(sums[c0][:], terms[c0][:, :, 0, :], terms[c0][:, :, 1, :], ADD)
+        def add_by_transposes(c, turns, banks, slot, back_bank):
+            across = [psum.tile([P, P], F32, name=f"across{c}{h}", tag=banks[h]) for h in range(2)]
+            for d in range(turns):
+                for h in range(2):
+                    nc.tensor.matmul(
+                        across[h][:],
+                        terms[c, d][:, h * P : (h + 1) * P],
+                        ident[:],
+                        start=(d == 0),
+                        stop=(d == turns - 1),
+                        is_transpose=True,
+                    )
+            summed = keep.tile([P, 2, P], F32, name=f"summed{c}", tag=slot, align_bytes=64)
+            for h in range(2):
+                nc.scalar.copy(summed[:, h, :], across[h][:])
+            back = psum.tile([P, V], F32, name=f"back{c}", tag=back_bank)
+            for h in range(2):
+                nc.tensor.transpose(back[:, h * P : (h + 1) * P], summed[:, h, :], ident[:])
+            return back
 
-        def add_last(c0, count):
-            nc.vector.tensor_tensor(outs[c0][:], sums[c0][:], terms[c0][:, :, 2, :], ADD)
-            rows = out[c0 * P : (c0 + count) * P, :]
-            nc.sync.dma_start(rows.rearrange("(c p) v -> p c v", p=P), outs[c0][:])
+        def store_from_bank(c, back):
+            result = keep.tile([P, V], F32, name=f"result{c}")
+            nc.scalar.copy(result[:], back[:])
+            nc.scalar.dma_start(out[c * P : (c + 1) * P, :], result[:])
 
-        fetch(0, 0, 0)
-        fetch(0, 1, 0)
-        prepare_w(2, 2, True)
-        results(2, [(0, S)])
-        results(3, [(0, S)])
-        fetch(0, 2, 0)
-        for d in range(D):
-            fetch(1, d, 0)
-        fetch(2, 0, 2)
-        add_first(0)
-        fetch(2, 1, 2)
-        add_last(0, 2)
-        fetch(2, 2, 2)
-        fetch(3, 0, 3)
-        add_first(2)
-        fetch(3, 1, 3)
-        fetch(3, 2, 3)
-        add_first(3)
-        add_last(2, 1)
-        add_last(3, 1)
+        def add_and_store(c, left, right, slot, queue):
+            result = keep.tile([P, V], F32, name=f"result{c}", tag=slot, align_bytes=64)
+            nc.vector.tensor_tensor(result[:], left, right, ADD)
+            queue.dma_start(out[c * P : (c + 1) * P, :], result[:])
+
+        for c in range(BLOCKS):
+            for d in range(D):
+                fetch(c, d)
+        back0 = add_by_transposes(0, D, ("spread0", "spread2"), "wq21", "acc3")
+        back1 = add_by_transposes(1, D, ("piece128", "piece256"), "wq31", "acc2")
+        store_from_bank(0, back0)
+        back2 = add_by_transposes(2, D - 1, ("spread0", "spread2"), "ws31", "acc0")
+        store_from_bank(1, back1)
+        first = keep.tile([P, V], F32, name="first")
+        nc.vector.tensor_tensor(first[:], terms[3, 0][:], terms[3, 1][:], ADD)
+        add_and_store(2, back2[:], terms[2, 2][:], "result2", nc.scalar)
+        add_and_store(3, first[:], terms[3, 2][:], "ws31", nc.sync)

@@ -38,10 +38,6 @@ def tile_picked_sub_lin_silu_sub_e_kernel(tc, xT, w, b, gate, offs, pos1, pos2, 
         nc.gpsimd.memset(rows_sb[:], 0.0)
         ident = keep.tile([P, P], F32, name="ident")
         make_identity(nc, ident[:])
-        warm = keep.tile([P, 8], F32, name="warm")
-        nc.gpsimd.memset(warm[:], 0.0)
-        warmed = keep.tile([P, 8], F32, name="warmed")
-        nc.scalar.activation(warmed[:], warm[:], SILU)
 
         def load_bias():
             nc.sync.dma_start(rows_sb[0:D, :], gate[:, 0, :])

@@ -22,7 +22,7 @@ K_PASS = P * PACK
 PASSES = K // K_PASS
 BLOCKS = N // P
 HALVES = [(0, S // 2), (S // 2, S)]
-PIECES = [(0, 128), (128, 256), (256, 512)]
+QUARTERS = [(i * S // 4, (i + 1) * S // 4) for i in range(4)]
 
 
 def tile_picked_sub_lin_silu_sub_e_kernel(tc, xT, w, b, gate, offs, pos1, pos2, pos3, out):
@@ -32,55 +32,100 @@ def tile_picked_sub_lin_silu_sub_e_kernel(tc, xT, w, b, gate, offs, pos1, pos2, 
         keep = ctx.enter_context(tc.tile_pool(name="keep", bufs=1))
         psum = ctx.enter_context(tc.psum_pool(name="psum", bufs=1))
 
+        placed = ctx.enter_context(tc.tile_pool(name="placed", bufs=1))
+        offsets = {
+            "y1": 0,
+            "wraw20": 1984,
+            "term02": 3968,
+            "y2": 5120,
+            "wraw31": 7104,
+            "summed0": 7168,
+            "term12": 9088,
+        }
+
+        def tile(shape, dtype, name, slot=None):
+            if name in offsets:
+                return placed.tile(shape, dtype, name=name, offset=offsets[name], align_bytes=64)
+            return keep.tile(shape, dtype, name=name, tag=slot or name, align_bytes=64)
+
         offs_sb = lists.tile([P, S // 16], U16, name="offs_sb")
-
-        rows_sb = keep.tile([P, V], F32, name="rows_sb")
-        nc.gpsimd.memset(rows_sb[:], 0.0)
-        ident = keep.tile([P, P], F32, name="ident")
-        make_identity(nc, ident[:])
-
-        def load_bias():
-            nc.sync.dma_start(rows_sb[0:D, :], gate[:, 0, :])
-            nc.sync.dma_start(rows_sb[4:6, :], b.rearrange("(r i) o -> r (i o)", i=V))
-
+        rows_sb = tile([P, 2, P], F32, "rows_sb")
+        rows_flat = rows_sb[:].rearrange("p h v -> p (h v)")
+        nc.gpsimd.memset(rows_flat[0:64, :], 0.0)
+        x_rows = xT.rearrange("(a p j) t -> p a j t", a=PASSES, j=PACK)
         planes = {}
-        for a, j0, count in ((0, 0, 1), (0, 1, 1), (0, 2, 1), (0, 3, 1), (1, 0, 1), (1, 1, 1), (1, 2, 1), (1, 3, 1)):
-            if (a, j0) == (1, 0):
-                load_bias()
-            rows = xT[a * K_PASS : (a + 1) * K_PASS, :].rearrange("(p j) t -> p j t", j=PACK)
-            group = keep.tile([P, count, T], F32, name=f"x{a}{j0}")
-            nc.sync.dma_start(group[:], rows[:, j0 : j0 + count, :])
-            if (a, j0) == (0, 0):
-                nc.sync.dma_start(offs_sb[:], offs)
+
+        def load_x(a, j0, count):
+            group = tile([P, count, T], F32, f"x{a}{j0}")
+            nc.sync.dma_start(group[:], x_rows[:, a, j0 : j0 + count, :])
             for j in range(count):
                 planes[a, j0 + j] = group[:, j, :]
 
+        load_x(0, 0, 2)
+        nc.sync.dma_start(offs_sb[:], offs)
+        nc.sync.dma_start(rows_flat[0:D, :], gate[:, 0, :])
+        nc.sync.dma_start(rows_flat[4:6, :], b.rearrange("(r i) o -> r (i o)", i=V))
+        load_x(0, 2, 2)
+        for j in range(PACK):
+            load_x(1, j, 1)
+
         raws = {}
 
-        def load_w(a, c, blocks):
-            raw = keep.tile([P, PACK, blocks * P], F32, name=f"wraw{a}{c}", align_bytes=64)
-            rows = w[a * K_PASS : (a + 1) * K_PASS, c * P : (c + blocks) * P]
+        def load_w(c, a):
+            raw = tile([P, PACK, P], F32, f"wraw{c}{a}")
+            rows = w[a * K_PASS : (a + 1) * K_PASS, c * P : (c + 1) * P]
             nc.sync.dma_start(raw[:], rows.rearrange("(p j) m -> p j m", j=PACK))
-            raws[a, c] = raw
+            raws[c, a] = raw
+
+        pos_sb = []
+
+        def load_pos(pos):
+            pos_tile = lists.tile([P, V // 16], U16, name=f"pos_sb{len(pos_sb)}")
+            nc.sync.dma_start(pos_tile[:], pos)
+            pos_sb.append(pos_tile)
 
         for c in (0, 1):
             for a in range(PASSES):
-                load_w(a, c, 1)
-        pos_sb = []
-        for d, pos in enumerate((pos1, pos2, pos3)):
-            pos_tile = lists.tile([P, V // 16], U16, name=f"pos_sb{d}")
-            nc.sync.dma_start(pos_tile[:], pos)
-            pos_sb.append(pos_tile)
-        for c in (2, 3):
-            for a in range(PASSES):
-                load_w(a, c, 1)
+                load_w(c, a)
+        load_pos(pos1)
+        load_w(2, 0)
+        load_pos(pos2)
+        load_pos(pos3)
+        load_w(2, 1)
+        load_w(3, 0)
+        load_w(3, 1)
 
-        xb, xq, xs = [], [], []
-        for a in range(PASSES):
-            xb.append(keep.tile([P, S, PACK], BF16, name=f"xb{a}", align_bytes=64))
-            xs.append(keep.tile([P, S], U8, name=f"xs{a}", align_bytes=64))
-        xq.append(keep.tile([P, S], U32, name="xq0", align_bytes=64))
-        picked = [keep.tile([P, PACK, S], F32, name=f"picked{a}") for a in range(PASSES)]
+        ident = tile([P, P], F32, "ident")
+        make_identity(nc, ident[:])
+        for h in range(2):
+            nc.scalar.activation(rows_sb[64:P, h, :], ident[64:P, :], SILU, scale=0.0)
+        turned = psum.tile([P, 2, P], F32, name="turned", tag="C0")
+        for h in range(2):
+            nc.tensor.transpose(turned[:, h, :], rows_sb[:, h, :], ident[:])
+        cols = tile([P, 2, 8], F32, "cols")
+        nc.scalar.copy(cols[:], turned[:, :, 0:8])
+        gate_sb = tile([P, D, V], F32, "gate_sb")
+        for d0, count in ((0, 2), (2, 1)):
+            spread = psum.tile([P, count, V], F32, name=f"spread{d0}", tag=f"B{d0 // 2}")
+            for d in range(count):
+                for h in range(2):
+                    nc.tensor.transpose(
+                        spread[:, d, h * P : (h + 1) * P],
+                        cols[:, h, d0 + d : d0 + d + 1].to_broadcast([P, P]),
+                        ident[:],
+                    )
+            nc.scalar.copy(gate_sb[:, d0 : d0 + count, :], spread[:])
+
+        xb = [tile([P, S, PACK], BF16, f"xb{a}") for a in range(PASSES)]
+        xs = [tile([P, S], U8, f"xs{a}") for a in range(PASSES)]
+        whole = tile([P, S], U32, "xq0", "x11")
+        xq = {(0, lo): whole[:, lo:hi] for lo, hi in HALVES}
+
+        def codes(a, lo, hi):
+            start = lo // (S // 2) * (S // 2)
+            return xq[a, start][:, lo - start : hi - start].bitcast(FP8X4)
+
+        picked = [tile([P, PACK, S], F32, f"picked{a}") for a in range(PASSES)]
 
         def gather_wide(a, j):
             nc.vector.tensor_copy(picked[a][:, j, :], planes[a, j].indirect(offs_sb[:]))
@@ -90,115 +135,77 @@ def tile_picked_sub_lin_silu_sub_e_kernel(tc, xT, w, b, gate, offs, pos1, pos2, 
 
         def interleave_x(a, j0, j1, lo, hi):
             nc.scalar.copy(
-                xb[a][:, lo:hi, j0:j1], picked[a][:, j0:j1, lo:hi].rearrange("p j s -> p s j")
+                xb[a][:, lo:hi, j0:j1].rearrange("p (g i) j -> p g j i", i=4),
+                picked[a][:, j0:j1, lo:hi].rearrange("p j (g i) -> p g j i", i=4),
             )
 
         def quantise_x(a, lo, hi):
             nc.vector.quantize_mx(
-                out=xq[a][:, lo:hi].bitcast(FP8X4),
+                out=whole[:].bitcast(FP8X4) if a == 0 else codes(a, lo, hi),
                 scales=xs[a][:, lo:hi],
                 in_=xb[a][:, lo:hi, :].rearrange("p s j -> p (s j)"),
             )
 
         for j in range(PACK):
             gather_wide(0, j)
-        for lo in (0, S // 2):
-            interleave_x(0, 0, PACK, lo, lo + S // 2)
-        turned = psum.tile([P, 2, P], F32, name="turned", tag="acc3")
-        for h in range(2):
-            nc.tensor.transpose(turned[:, h, :], rows_sb[:, h * P : (h + 1) * P], ident[:])
-        cols = keep.tile([P, 2, 8], F32, name="cols")
-        nc.scalar.copy(cols[:], turned[:, :, 0:8])
-        gate_sb = keep.tile([P, D, V], F32, name="gate_sb")
-        for d0, count in ((0, 2), (2, 1)):
-            spread = psum.tile([P, count, V], F32, name=f"spread{d0}")
-            for d in range(count):
-                for h in range(2):
-                    nc.tensor.transpose(
-                        spread[:, d, h * P : (h + 1) * P],
-                        cols[:, h, d0 + d : d0 + d + 1].to_broadcast([P, P]),
-                        ident[:],
-                    )
-            nc.scalar.copy(gate_sb[:, d0 : d0 + count, :], spread[:])
+        for lo, hi in HALVES:
+            interleave_x(0, 0, PACK, lo, hi)
         gather_wide(1, 0)
         gather_wide(1, 1)
-        interleave_x(1, 0, 2, 0, S)
+        for lo, hi in HALVES:
+            interleave_x(1, 0, 2, lo, hi)
         quantise_x(0, 0, S)
-        gather(1, 2, 0, S)
+        for lo, hi in HALVES:
+            gather(1, 2, lo, hi)
         gather(1, 3, 0, S)
-        weights = {}
 
-        def interleave_w(dst, a, c):
-            copy = nc.vector.tensor_copy if c == 1 else nc.scalar.copy
+        woven, weights = {}, {}
+
+        def weave_w(c, a, copy, slot=None):
+            wb = tile([P, P, PACK], BF16, f"wb{c}{a}", slot)
             copy(
-                dst.rearrange("p (g i) j -> p g j i", i=4),
-                raws[a, c][:].rearrange("p j (g i) -> p g j i", i=4),
+                wb[:].rearrange("p (g i) j -> p g j i", i=4),
+                raws[c, a][:].rearrange("p j (g i) -> p g j i", i=4),
             )
+            woven[c, a] = wb
 
-        def prepare_pass(c, a, slot):
-            wq = keep.tile([P, P], U32, name=f"wq{c}{a}", align_bytes=64)
-            ws = keep.tile([P, P], U8, name=f"ws{c}{a}", align_bytes=64)
-            wb = keep.tile([P, P, PACK], BF16, name=f"wb{c}{a}", tag=slot, align_bytes=64)
-            interleave_w(wb[:], a, c)
-            nc.vector.quantize_mx(out=wq[:].bitcast(FP8X4), scales=ws[:], in_=wb[:].rearrange("p m j -> p (m j)"))
+        def quantise_w(c, a):
+            wq = tile([P, P], U32, f"wq{c}{a}")
+            ws = tile([P, P], U8, f"ws{c}{a}")
+            nc.vector.quantize_mx(
+                out=wq[:].bitcast(FP8X4), scales=ws[:], in_=woven[c, a][:].rearrange("p m j -> p (m j)")
+            )
             weights[c, a] = (wq[:], ws[:])
 
-        def prepare_w(c, slot):
-            wq = keep.tile([P, PASSES, P], U32, name=f"wq{c}", align_bytes=64)
-            ws = keep.tile([P, PASSES, P], U8, name=f"ws{c}", align_bytes=64)
-            wb = keep.tile([P, PASSES, P, PACK], BF16, name=f"wb{c}", tag=slot, align_bytes=64)
-            for a in range(PASSES):
-                interleave_w(wb[:, a], a, c)
-            nc.vector.quantize_mx(
-                out=wq[:].rearrange("p a m -> p (a m)").bitcast(FP8X4),
-                scales=ws[:].rearrange("p a m -> p (a m)"),
-                in_=wb[:].rearrange("p a m j -> p (a m j)"),
-            )
-            for a in range(PASSES):
-                weights[c, a] = (wq[:, a, :], ws[:, a, :])
+        ys = {}
 
-        def results(c, pieces, banks):
-            y = keep.tile([P, S], F32, name=f"y{c}", tag="wraw12" if c == 1 else f"y{c}", align_bytes=64)
-            for (lo, hi), bank in zip(pieces, banks):
-                acc = psum.tile([P, hi - lo], F32, name=f"acc{c}{lo}", tag=bank)
+        def results(c, pieces, banks, slot=None):
+            y = tile([P, S], F32, f"y{c}", slot)
+            accs = [psum.tile([P, hi - lo], F32, name=f"acc{c}{lo}", tag=bank) for (lo, hi), bank in zip(pieces, banks)]
+            for (lo, hi), acc in zip(pieces, accs):
                 for a in range(PASSES):
                     wq, ws = weights[c, a]
                     nc.tensor.matmul_mx(
                         out=acc[:],
                         lhsT=wq.bitcast(FP8X4),
                         lhsT_scale=ws,
-                        rhs=xq[a][:, lo:hi].bitcast(FP8X4),
+                        rhs=codes(a, lo, hi),
                         rhs_scale=xs[a][:, lo:hi],
                         start=(a == 0),
                         stop=(a == PASSES - 1),
                     )
+            for (lo, hi), acc in zip(pieces, accs):
                 nc.scalar.activation(y[:, lo:hi], acc[:], SILU, bias=cols[:, c % 2, 4 + c // 2 : 5 + c // 2])
-            ys.append(y)
-
-        ys = []
-        prepare_pass(0, 0, "wb00")
-        xq.append(keep.tile([P, S], U32, name="xq1", tag="wraw00", align_bytes=64))
-        quantise_x(1, 0, S)
-        prepare_pass(0, 1, "wb01")
-        results(0, PIECES, ("acc0", "piece128", "piece256"))
-        prepare_w(1, "wraw10")
-        prepare_pass(2, 0, "wq01")
-        prepare_pass(2, 1, "wb21")
-        results(1, [(0, S)], ("acc1",))
-        prepare_pass(3, 0, "wq1")
-        prepare_pass(3, 1, "wb31")
-        results(2, HALVES, ("acc2", "acc0"))
-        results(3, HALVES, ("acc3", "acc1"))
+            ys[c] = y
 
         terms = {}
-        slots = {(0, 2): "wraw02", (1, 1): "wraw03", (1, 2): "wraw13"}
 
-        def fetch(c, d):
-            term = keep.tile([P, V], F32, name=f"term{c}{d}", tag=slots.get((c, d), f"term{c}{d}"), align_bytes=64)
+        def fetch(c, d, slot=None):
+            term = tile([P, V], F32, f"term{c}{d}", slot)
             nc.vector.tensor_tensor(term[:], ys[c][:].indirect(pos_sb[d][:]), gate_sb[:, d, :], MULT)
             terms[c, d] = term
 
-        def add_by_transposes(c, turns, banks, slot, back_bank):
+        def turn_and_add(c, banks, turns=D):
             across = [psum.tile([P, P], F32, name=f"across{c}{h}", tag=banks[h]) for h in range(2)]
             for d in range(turns):
                 for h in range(2):
@@ -210,33 +217,69 @@ def tile_picked_sub_lin_silu_sub_e_kernel(tc, xT, w, b, gate, offs, pos1, pos2, 
                         stop=(d == turns - 1),
                         is_transpose=True,
                     )
-            summed = keep.tile([P, 2, P], F32, name=f"summed{c}", tag=slot, align_bytes=64)
+            return across
+
+        def turn_back(c, across, bank, slot=None):
+            summed = tile([P, 2, P], F32, f"summed{c}", slot)
             for h in range(2):
                 nc.scalar.copy(summed[:, h, :], across[h][:])
-            back = psum.tile([P, V], F32, name=f"back{c}", tag=back_bank)
+            back = psum.tile([P, V], F32, name=f"back{c}", tag=bank)
             for h in range(2):
                 nc.tensor.transpose(back[:, h * P : (h + 1) * P], summed[:, h, :], ident[:])
             return back
 
-        def store_from_bank(c, back):
-            result = keep.tile([P, V], F32, name=f"result{c}")
+        def store_from_bank(c, back, slot=None):
+            result = tile([P, V], F32, f"result{c}", slot)
             nc.scalar.copy(result[:], back[:])
             nc.scalar.dma_start(out[c * P : (c + 1) * P, :], result[:])
 
-        def add_and_store(c, left, right, slot, queue):
-            result = keep.tile([P, V], F32, name=f"result{c}", tag=slot, align_bytes=64)
+        for a in range(PASSES):
+            weave_w(0, a, nc.scalar.copy)
+            quantise_w(0, a)
+            xq[1, a * S // 2] = tile([P, S // 2], U32, f"xq1{a}", f"wraw0{a}")[:]
+            for lo, hi in QUARTERS[2 * a : 2 * a + 2]:
+                quantise_x(1, lo, hi)
+        weave_w(1, 0, nc.scalar.copy)
+        weave_w(1, 1, nc.vector.tensor_copy)
+        results(0, QUARTERS, ("A0", "A1", "A2", "A3"), "wraw10")
+        for a in range(PASSES):
+            quantise_w(1, a)
+        weave_w(2, 0, nc.scalar.copy, "wq01")
+        results(1, HALVES, ("B0", "B1"))
+        fetch(0, 0, "wraw11")
+        fetch(0, 1)
+        quantise_w(2, 0)
+        fetch(0, 2)
+        weave_w(2, 1, nc.scalar.copy, "wq11")
+        weave_w(3, 0, nc.scalar.copy, "ws11")
+        weave_w(3, 1, nc.scalar.copy, "wq10")
+        quantise_w(2, 1)
+        results(2, HALVES, ("C0", "C1"))
+        across0 = turn_and_add(0, ("C0", "C1"))
+        fetch(1, 0, "wraw21")
+        quantise_w(3, 0)
+        fetch(1, 1, "wraw30")
+        quantise_w(3, 1)
+        fetch(1, 2)
+        back0 = turn_back(0, across0, "C0")
+        results(3, HALVES, ("A0", "A1"))
+        across1 = turn_and_add(1, ("A2", "A3"))
+        for d in range(D):
+            fetch(2, d)
+        across2 = turn_and_add(2, ("B0", "B1"), D - 1)
+        back2 = turn_back(2, across2, "A0", "ws31")
+        back1 = turn_back(1, across1, "B0", "wq31")
+        store_from_bank(0, back0)
+        store_from_bank(1, back1)
+
+        def add_and_store(c, left, right, queue, slot=None):
+            result = tile([P, V], F32, f"result{c}", slot)
             nc.vector.tensor_tensor(result[:], left, right, ADD)
             queue.dma_start(out[c * P : (c + 1) * P, :], result[:])
 
-        for c in range(BLOCKS):
-            for d in range(D):
-                fetch(c, d)
-        back0 = add_by_transposes(0, D, ("spread0", "spread2"), "wq21", "acc3")
-        back1 = add_by_transposes(1, D, ("piece128", "piece256"), "wq31", "acc2")
-        store_from_bank(0, back0)
-        back2 = add_by_transposes(2, D - 1, ("spread0", "spread2"), "ws31", "acc0")
-        store_from_bank(1, back1)
-        first = keep.tile([P, V], F32, name="first")
-        nc.vector.tensor_tensor(first[:], terms[3, 0][:], terms[3, 1][:], ADD)
-        add_and_store(2, back2[:], terms[2, 2][:], "result2", nc.scalar)
-        add_and_store(3, first[:], terms[3, 2][:], "ws31", nc.sync)
+        for d in range(D):
+            fetch(3, d)
+        pair = tile([P, V], F32, "pair")
+        nc.vector.tensor_tensor(pair[:], terms[3, 0][:], terms[3, 1][:], ADD)
+        add_and_store(2, back2[:], terms[2, 2][:], nc.sync)
+        add_and_store(3, pair[:], terms[3, 2][:], nc.sync, "ws31")

@@ -38,9 +38,11 @@ def tile_picked_sub_lin_silu_sub_e_kernel(tc, xT, w, b, gate, offs, pos1, pos2, 
             "wraw20": 1984,
             "term02": 3968,
             "y2": 5120,
-            "wraw31": 7104,
-            "summed0": 7168,
-            "term12": 9088,
+            "wraw30": 7104,
+            "term11": 9088,
+            "wraw31": 10240,
+            "summed0": 10240,
+            "term12": 11264,
         }
 
         def tile(shape, dtype, name, slot=None):
@@ -255,21 +257,21 @@ def tile_picked_sub_lin_silu_sub_e_kernel(tc, xT, w, b, gate, offs, pos1, pos2, 
         weave_w(3, 1, nc.scalar.copy, "wq10")
         quantise_w(2, 1)
         results(2, HALVES, ("C0", "C1"))
-        across0 = turn_and_add(0, ("C0", "C1"))
+        across0 = turn_and_add(0, ("B0", "B1"))
         fetch(1, 0, "wraw21")
         quantise_w(3, 0)
-        fetch(1, 1, "wraw30")
+        fetch(1, 1)
         quantise_w(3, 1)
         fetch(1, 2)
-        back0 = turn_back(0, across0, "C0")
+        back0 = turn_back(0, across0, "B0")
         results(3, HALVES, ("A0", "A1"))
         across1 = turn_and_add(1, ("A2", "A3"))
         for d in range(D):
             fetch(2, d)
-        across2 = turn_and_add(2, ("B0", "B1"), D - 1)
+        across2 = turn_and_add(2, ("C0", "C1"), D - 1)
         back2 = turn_back(2, across2, "A0", "ws31")
-        back1 = turn_back(1, across1, "B0", "wq31")
-        store_from_bank(0, back0)
+        back1 = turn_back(1, across1, "B1", "wq31")
+        store_from_bank(0, back0, "wraw01")
         store_from_bank(1, back1)
 
         def add_and_store(c, left, right, queue, slot=None):

@@ -163,20 +163,26 @@ def tile_picked_sub_lin_silu_sub_e_kernel(tc, xT, w, b, gate, offs, pos1, pos2, 
 
         woven, weights = {}, {}
 
-        def weave_w(c, a, copy, slot=None):
+        def weave_w(c, a, copy, slot=None, parts=1):
             wb = tile([P, P, PACK], BF16, f"wb{c}{a}", slot)
-            copy(
-                wb[:].rearrange("p (g i) j -> p g j i", i=4),
-                raws[c, a][:].rearrange("p j (g i) -> p g j i", i=4),
-            )
+            for part in range(parts):
+                channels = slice(part * P // parts, (part + 1) * P // parts)
+                copy(
+                    wb[:, channels, :].rearrange("p (g i) j -> p g j i", i=4),
+                    raws[c, a][:, :, channels].rearrange("p j (g i) -> p g j i", i=4),
+                )
             woven[c, a] = wb
 
-        def quantise_w(c, a):
+        def quantise_w(c, a, parts=1):
             wq = tile([P, P], U32, f"wq{c}{a}")
             ws = tile([P, P], U8, f"ws{c}{a}")
-            nc.vector.quantize_mx(
-                out=wq[:].bitcast(FP8X4), scales=ws[:], in_=woven[c, a][:].rearrange("p m j -> p (m j)")
-            )
+            for part in range(parts):
+                channels = slice(part * P // parts, (part + 1) * P // parts)
+                nc.vector.quantize_mx(
+                    out=wq[:, channels].bitcast(FP8X4),
+                    scales=ws[:, channels],
+                    in_=woven[c, a][:, channels, :].rearrange("p m j -> p (m j)"),
+                )
             weights[c, a] = (wq[:], ws[:])
 
         ys = {}
@@ -221,10 +227,13 @@ def tile_picked_sub_lin_silu_sub_e_kernel(tc, xT, w, b, gate, offs, pos1, pos2, 
                     )
             return across
 
-        def turn_back(c, across, bank, slot=None):
+        def copy_sum(c, across, slot=None):
             summed = tile([P, 2, P], F32, f"summed{c}", slot)
             for h in range(2):
                 nc.scalar.copy(summed[:, h, :], across[h][:])
+            return summed
+
+        def turn_back(c, summed, bank):
             back = psum.tile([P, V], F32, name=f"back{c}", tag=bank)
             for h in range(2):
                 nc.tensor.transpose(back[:, h * P : (h + 1) * P], summed[:, h, :], ident[:])
@@ -242,10 +251,10 @@ def tile_picked_sub_lin_silu_sub_e_kernel(tc, xT, w, b, gate, offs, pos1, pos2, 
             for lo, hi in QUARTERS[2 * a : 2 * a + 2]:
                 quantise_x(1, lo, hi)
         weave_w(1, 0, nc.scalar.copy)
-        weave_w(1, 1, nc.vector.tensor_copy)
+        weave_w(1, 1, nc.vector.tensor_copy, parts=2)
         results(0, QUARTERS, ("A0", "A1", "A2", "A3"), "wraw10")
-        for a in range(PASSES):
-            quantise_w(1, a)
+        quantise_w(1, 0)
+        quantise_w(1, 1, parts=2)
         weave_w(2, 0, nc.scalar.copy, "wq01")
         results(1, HALVES, ("B0", "B1"))
         fetch(0, 0, "wraw11")
@@ -263,25 +272,28 @@ def tile_picked_sub_lin_silu_sub_e_kernel(tc, xT, w, b, gate, offs, pos1, pos2, 
         fetch(1, 1)
         quantise_w(3, 1)
         fetch(1, 2)
-        back0 = turn_back(0, across0, "B0")
+        summed0 = copy_sum(0, across0)
         results(3, HALVES, ("A0", "A1"))
         across1 = turn_and_add(1, ("A2", "A3"))
         for d in range(D):
             fetch(2, d)
         across2 = turn_and_add(2, ("C0", "C1"), D - 1)
-        back2 = turn_back(2, across2, "A0", "ws31")
-        back1 = turn_back(1, across1, "B1", "wq31")
-        store_from_bank(0, back0, "wraw01")
+        back2 = turn_back(2, copy_sum(2, across2, "ws31"), "A0")
+        back0 = turn_back(0, summed0, "A1")
+        back1 = turn_back(1, copy_sum(1, across1, "wq31"), "B1")
+        store_from_bank(0, back0, "term21")
         store_from_bank(1, back1)
-
-        def add_and_store(c, left, right, queue, slot=None):
-            result = tile([P, V], F32, f"result{c}", slot)
-            nc.vector.tensor_tensor(result[:], left, right, ADD)
-            queue.dma_start(out[c * P : (c + 1) * P, :], result[:])
 
         for d in range(D):
             fetch(3, d)
         pair = tile([P, V], F32, "pair")
-        nc.vector.tensor_tensor(pair[:], terms[3, 0][:], terms[3, 1][:], ADD)
-        add_and_store(2, back2[:], terms[2, 2][:], nc.sync)
-        add_and_store(3, pair[:], terms[3, 2][:], nc.sync, "ws31")
+        result3 = tile([P, V], F32, "result3")
+        targets = [slice(0, P), slice(P, V)]
+        for half in targets:
+            nc.vector.tensor_tensor(pair[:, half], terms[3, 0][:, half], terms[3, 1][:, half], ADD)
+        for half in targets:
+            nc.vector.tensor_tensor(result3[:, half], pair[:, half], terms[3, 2][:, half], ADD)
+        nc.sync.dma_start(out[3 * P : 4 * P, :], result3[:])
+        result2 = tile([P, V], F32, "result2")
+        nc.vector.tensor_tensor(result2[:], back2[:], terms[2, 2][:], ADD)
+        nc.sync.dma_start(out[2 * P : 3 * P, :], result2[:])

@@ -89,11 +89,11 @@ def tile_picked_sub_lin_silu_sub_e_kernel(tc, xT, w, b, gate, offs, pos1, pos2, 
         for c in (0, 1):
             for a in range(PASSES):
                 load_w(c, a)
-        load_pos(pos1)
         load_w(2, 0)
+        load_pos(pos1)
         load_pos(pos2)
-        load_pos(pos3)
         load_w(2, 1)
+        load_pos(pos3)
         load_w(3, 0)
         load_w(3, 1)
 

@@ -213,16 +213,16 @@ def tile_picked_sub_lin_silu_sub_e_kernel(tc, xT, w, b, gate, offs, pos1, pos2, 
             nc.vector.tensor_tensor(term[:], ys[c][:].indirect(pos_sb[d][:]), gate_sb[:, d, :], MULT)
             terms[c, d] = term
 
-        def turn_and_add(c, banks, turns=D):
+        def turn_and_add(c, banks, order=range(D)):
             across = [psum.tile([P, P], F32, name=f"across{c}{h}", tag=banks[h]) for h in range(2)]
-            for d in range(turns):
+            for d in order:
                 for h in range(2):
                     nc.tensor.matmul(
                         across[h][:],
                         terms[c, d][:, h * P : (h + 1) * P],
                         ident[:],
-                        start=(d == 0),
-                        stop=(d == turns - 1),
+                        start=(d == order[0]),
+                        stop=(d == order[-1]),
                         is_transpose=True,
                     )
             return across
@@ -274,10 +274,10 @@ def tile_picked_sub_lin_silu_sub_e_kernel(tc, xT, w, b, gate, offs, pos1, pos2, 
         fetch(1, 2)
         summed0 = copy_sum(0, across0)
         results(3, HALVES, ("A0", "A1"))
-        across1 = turn_and_add(1, ("A2", "A3"))
+        across1 = turn_and_add(1, ("A2", "A3"), (2, 0, 1))
         for d in range(D):
             fetch(2, d)
-        across2 = turn_and_add(2, ("C0", "C1"), D - 1)
+        across2 = turn_and_add(2, ("C0", "C1"), (0, 1))
         back2 = turn_back(2, copy_sum(2, across2, "ws31"), "A0")
         back0 = turn_back(0, summed0, "A1")
         back1 = turn_back(1, copy_sum(1, across1, "wq31"), "B1")
@@ -287,13 +287,10 @@ def tile_picked_sub_lin_silu_sub_e_kernel(tc, xT, w, b, gate, offs, pos1, pos2, 
         for d in range(D):
             fetch(3, d)
         pair = tile([P, V], F32, "pair")
-        result3 = tile([P, V], F32, "result3")
-        targets = [slice(0, P), slice(P, V)]
-        for half in targets:
-            nc.vector.tensor_tensor(pair[:, half], terms[3, 0][:, half], terms[3, 1][:, half], ADD)
-        for half in targets:
-            nc.vector.tensor_tensor(result3[:, half], pair[:, half], terms[3, 2][:, half], ADD)
-        nc.sync.dma_start(out[3 * P : 4 * P, :], result3[:])
+        nc.vector.tensor_tensor(pair[:], terms[3, 0][:], terms[3, 1][:], ADD)
         result2 = tile([P, V], F32, "result2")
         nc.vector.tensor_tensor(result2[:], back2[:], terms[2, 2][:], ADD)
         nc.sync.dma_start(out[2 * P : 3 * P, :], result2[:])
+        result3 = tile([P, V], F32, "result3", "ws31")
+        nc.vector.tensor_tensor(result3[:], pair[:], terms[3, 2][:], ADD)
+        nc.sync.dma_start(out[3 * P : 4 * P, :], result3[:])

@@ -242,7 +242,7 @@ def tile_picked_sub_lin_silu_sub_e_kernel(tc, xT, w, b, gate, offs, pos1, pos2, 
         def store_from_bank(c, back, slot=None):
             result = tile([P, V], F32, f"result{c}", slot)
             nc.scalar.copy(result[:], back[:])
-            nc.scalar.dma_start(out[c * P : (c + 1) * P, :], result[:])
+            nc.sync.dma_start(out[c * P : (c + 1) * P, :], result[:])
 
         for a in range(PASSES):
             weave_w(0, a, nc.scalar.copy)

from contextlib import ExitStack

import concourse.mybir as mybir
from concourse.masks import make_identity

K, T, D, S, V, N = 1024, 2048, 3, 512, 256, 512
FLOPS = 2 * K * S * N

F32 = mybir.dt.float32
BF16 = mybir.dt.bfloat16
U32 = mybir.dt.uint32
U16 = mybir.dt.uint16
U8 = mybir.dt.uint8
FP8X4 = mybir.dt.float8_e4m3fn_x4
MULT = mybir.AluOpType.mult
ADD = mybir.AluOpType.add
SILU = mybir.ActivationFunctionType.Silu

P = 128
PACK = 4
K_PASS = P * PACK
PASSES = K // K_PASS
BLOCKS = N // P
HALVES = [(0, S // 2), (S // 2, S)]
QUARTERS = [(i * S // 4, (i + 1) * S // 4) for i in range(4)]


def tile_picked_sub_lin_silu_sub_e_kernel(tc, xT, w, b, gate, offs, pos1, pos2, pos3, out):
    nc = tc.nc
    with ExitStack() as ctx:
        lists = ctx.enter_context(tc.tile_pool(name="lists", bufs=1))
        keep = ctx.enter_context(tc.tile_pool(name="keep", bufs=1))
        psum = ctx.enter_context(tc.psum_pool(name="psum", bufs=1))

        placed = ctx.enter_context(tc.tile_pool(name="placed", bufs=1))
        offsets = {
            "y1": 0,
            "wraw20": 1984,
            "term02": 3968,
            "y2": 5120,
            "wraw30": 7104,
            "term11": 9088,
            "wraw31": 10240,
            "summed0": 10240,
            "term12": 11264,
        }

        def tile(shape, dtype, name, slot=None):
            if name in offsets:
                return placed.tile(shape, dtype, name=name, offset=offsets[name], align_bytes=64)
            return keep.tile(shape, dtype, name=name, tag=slot or name, align_bytes=64)

        offs_sb = lists.tile([P, S // 16], U16, name="offs_sb")
        rows_sb = tile([P, 2, P], F32, "rows_sb")
        rows_flat = rows_sb[:].rearrange("p h v -> p (h v)")
        nc.gpsimd.memset(rows_flat[0:64, :], 0.0)
        x_rows = xT.rearrange("(a p j) t -> p a j t", a=PASSES, j=PACK)
        planes = {}

        def load_x(a, j0, count):
            group = tile([P, count, T], F32, f"x{a}{j0}")
            nc.sync.dma_start(group[:], x_rows[:, a, j0 : j0 + count, :])
            for j in range(count):
                planes[a, j0 + j] = group[:, j, :]

        load_x(0, 0, 2)
        nc.sync.dma_start(offs_sb[:], offs)
        nc.sync.dma_start(rows_flat[0:D, :], gate[:, 0, :])
        nc.sync.dma_start(rows_flat[4:6, :], b.rearrange("(r i) o -> r (i o)", i=V))
        load_x(0, 2, 2)
        for j in range(PACK):
            load_x(1, j, 1)

        raws = {}

        def load_w(c, a):
            raw = tile([P, PACK, P], F32, f"wraw{c}{a}")
            rows = w[a * K_PASS : (a + 1) * K_PASS, c * P : (c + 1) * P]
            nc.sync.dma_start(raw[:], rows.rearrange("(p j) m -> p j m", j=PACK))
            raws[c, a] = raw

        pos_sb = []

        def load_pos(pos):
            pos_tile = lists.tile([P, V // 16], U16, name=f"pos_sb{len(pos_sb)}")
            nc.sync.dma_start(pos_tile[:], pos)
            pos_sb.append(pos_tile)

        for c in (0, 1):
            for a in range(PASSES):
                load_w(c, a)
        load_w(2, 0)
        load_pos(pos1)
        load_pos(pos2)
        load_w(2, 1)
        load_pos(pos3)
        load_w(3, 0)
        load_w(3, 1)

        ident = tile([P, P], F32, "ident")
        make_identity(nc, ident[:])
        for h in range(2):
            nc.scalar.activation(rows_sb[64:P, h, :], ident[64:P, :], SILU, scale=0.0)
        turned = psum.tile([P, 2, P], F32, name="turned", tag="C0")
        for h in range(2):
            nc.tensor.transpose(turned[:, h, :], rows_sb[:, h, :], ident[:])
        cols = tile([P, 2, 8], F32, "cols")
        nc.scalar.copy(cols[:], turned[:, :, 0:8])
        gate_sb = tile([P, D, V], F32, "gate_sb")
        for d0, count in ((0, 2), (2, 1)):
            spread = psum.tile([P, count, V], F32, name=f"spread{d0}", tag=f"B{d0 // 2}")
            for d in range(count):
                for h in range(2):
                    nc.tensor.transpose(
                        spread[:, d, h * P : (h + 1) * P],
                        cols[:, h, d0 + d : d0 + d + 1].to_broadcast([P, P]),
                        ident[:],
                    )
            nc.scalar.copy(gate_sb[:, d0 : d0 + count, :], spread[:])

        xb = [tile([P, S, PACK], BF16, f"xb{a}") for a in range(PASSES)]
        xs = [tile([P, S], U8, f"xs{a}") for a in range(PASSES)]
        whole = tile([P, S], U32, "xq0", "x11")
        xq = {(0, lo): whole[:, lo:hi] for lo, hi in HALVES}

        def codes(a, lo, hi):
            start = lo // (S // 2) * (S // 2)
            return xq[a, start][:, lo - start : hi - start].bitcast(FP8X4)

        picked = [tile([P, PACK, S], F32, f"picked{a}") for a in range(PASSES)]

        def gather_wide(a, j):
            nc.vector.tensor_copy(picked[a][:, j, :], planes[a, j].indirect(offs_sb[:]))

        def gather(a, j, lo, hi):
            nc.vector.tensor_copy(xb[a][:, lo:hi, j], planes[a, j].indirect(offs_sb[:, lo // 16 : hi // 16]))

        def interleave_x(a, j0, j1, lo, hi):
            nc.scalar.copy(
                xb[a][:, lo:hi, j0:j1].rearrange("p (g i) j -> p g j i", i=4),
                picked[a][:, j0:j1, lo:hi].rearrange("p j (g i) -> p g j i", i=4),
            )

        def quantise_x(a, lo, hi):
            nc.vector.quantize_mx(
                out=whole[:].bitcast(FP8X4) if a == 0 else codes(a, lo, hi),
                scales=xs[a][:, lo:hi],
                in_=xb[a][:, lo:hi, :].rearrange("p s j -> p (s j)"),
            )

        for j in range(PACK):
            gather_wide(0, j)
        for lo, hi in HALVES:
            interleave_x(0, 0, PACK, lo, hi)
        gather_wide(1, 0)
        gather_wide(1, 1)
        for lo, hi in HALVES:
            interleave_x(1, 0, 2, lo, hi)
        quantise_x(0, 0, S)
        for lo, hi in HALVES:
            gather(1, 2, lo, hi)
        gather(1, 3, 0, S)

        woven, weights = {}, {}

        def weave_w(c, a, copy, slot=None, parts=1):
            wb = tile([P, P, PACK], BF16, f"wb{c}{a}", slot)
            for part in range(parts):
                channels = slice(part * P // parts, (part + 1) * P // parts)
                copy(
                    wb[:, channels, :].rearrange("p (g i) j -> p g j i", i=4),
                    raws[c, a][:, :, channels].rearrange("p j (g i) -> p g j i", i=4),
                )
            woven[c, a] = wb

        def quantise_w(c, a, parts=1):
            wq = tile([P, P], U32, f"wq{c}{a}")
            ws = tile([P, P], U8, f"ws{c}{a}")
            for part in range(parts):
                channels = slice(part * P // parts, (part + 1) * P // parts)
                nc.vector.quantize_mx(
                    out=wq[:, channels].bitcast(FP8X4),
                    scales=ws[:, channels],
                    in_=woven[c, a][:, channels, :].rearrange("p m j -> p (m j)"),
                )
            weights[c, a] = (wq[:], ws[:])

        ys = {}

        def results(c, pieces, banks, slot=None):
            y = tile([P, S], F32, f"y{c}", slot)
            accs = [psum.tile([P, hi - lo], F32, name=f"acc{c}{lo}", tag=bank) for (lo, hi), bank in zip(pieces, banks)]
            for (lo, hi), acc in zip(pieces, accs):
                for a in range(PASSES):
                    wq, ws = weights[c, a]
                    nc.tensor.matmul_mx(
                        out=acc[:],
                        lhsT=wq.bitcast(FP8X4),
                        lhsT_scale=ws,
                        rhs=codes(a, lo, hi),
                        rhs_scale=xs[a][:, lo:hi],
                        start=(a == 0),
                        stop=(a == PASSES - 1),
                    )
            for (lo, hi), acc in zip(pieces, accs):
                nc.scalar.activation(y[:, lo:hi], acc[:], SILU, bias=cols[:, c % 2, 4 + c // 2 : 5 + c // 2])
            ys[c] = y

        terms = {}

        def fetch(c, d, slot=None):
            term = tile([P, V], F32, f"term{c}{d}", slot)
            nc.vector.tensor_tensor(term[:], ys[c][:].indirect(pos_sb[d][:]), gate_sb[:, d, :], MULT)
            terms[c, d] = term

        def turn_and_add(c, banks, order=range(D)):
            across = [psum.tile([P, P], F32, name=f"across{c}{h}", tag=banks[h]) for h in range(2)]
            for d in order:
                for h in range(2):
                    nc.tensor.matmul(
                        across[h][:],
                        terms[c, d][:, h * P : (h + 1) * P],
                        ident[:],
                        start=(d == order[0]),
                        stop=(d == order[-1]),
                        is_transpose=True,
                    )
            return across

        def copy_sum(c, across, slot=None):
            summed = tile([P, 2, P], F32, f"summed{c}", slot)
            for h in range(2):
                nc.scalar.copy(summed[:, h, :], across[h][:])
            return summed

        def turn_back(c, summed, bank):
            back = psum.tile([P, V], F32, name=f"back{c}", tag=bank)
            for h in range(2):
                nc.tensor.transpose(back[:, h * P : (h + 1) * P], summed[:, h, :], ident[:])
            return back

        def store_from_bank(c, back, slot=None):
            result = tile([P, V], F32, f"result{c}", slot)
            nc.scalar.copy(result[:], back[:])
            nc.sync.dma_start(out[c * P : (c + 1) * P, :], result[:])

        for a in range(PASSES):
            weave_w(0, a, nc.scalar.copy)
            quantise_w(0, a)
            xq[1, a * S // 2] = tile([P, S // 2], U32, f"xq1{a}", f"wraw0{a}")[:]
            for lo, hi in QUARTERS[2 * a : 2 * a + 2]:
                quantise_x(1, lo, hi)
        weave_w(1, 0, nc.scalar.copy)
        weave_w(1, 1, nc.vector.tensor_copy, parts=2)
        results(0, QUARTERS, ("A0", "A1", "A2", "A3"), "wraw10")
        quantise_w(1, 0)
        quantise_w(1, 1, parts=2)
        weave_w(2, 0, nc.scalar.copy, "wq01")
        results(1, HALVES, ("B0", "B1"))
        fetch(0, 0, "wraw11")
        fetch(0, 1)
        quantise_w(2, 0)
        fetch(0, 2)
        weave_w(2, 1, nc.scalar.copy, "wq11")
        weave_w(3, 0, nc.scalar.copy, "ws11")
        weave_w(3, 1, nc.scalar.copy, "wq10")
        quantise_w(2, 1)
        results(2, HALVES, ("C0", "C1"))
        across0 = turn_and_add(0, ("B0", "B1"))
        fetch(1, 0, "wraw21")
        quantise_w(3, 0)
        fetch(1, 1)
        quantise_w(3, 1)
        fetch(1, 2)
        summed0 = copy_sum(0, across0)
        results(3, HALVES, ("A0", "A1"))
        across1 = turn_and_add(1, ("A2", "A3"), (2, 0, 1))
        for d in range(D):
            fetch(2, d)
        across2 = turn_and_add(2, ("C0", "C1"), (0, 1))
        back2 = turn_back(2, copy_sum(2, across2, "ws31"), "A0")
        back0 = turn_back(0, summed0, "A1")
        back1 = turn_back(1, copy_sum(1, across1, "wq31"), "B1")
        store_from_bank(0, back0, "term21")
        store_from_bank(1, back1)

        for d in range(D):
            fetch(3, d)
        pair = tile([P, V], F32, "pair")
        nc.vector.tensor_tensor(pair[:], terms[3, 0][:], terms[3, 1][:], ADD)
        result2 = tile([P, V], F32, "result2")
        nc.vector.tensor_tensor(result2[:], back2[:], terms[2, 2][:], ADD)
        nc.sync.dma_start(out[2 * P : 3 * P, :], result2[:])
        result3 = tile([P, V], F32, "result3", "ws31")
        nc.vector.tensor_tensor(result3[:], pair[:], terms[3, 2][:], ADD)
        nc.sync.dma_start(out[3 * P : 4 * P, :], result3[:])
